import numpy as np
import ml_dtypes


def mxq(x, axis, fmt="e4m3"):
    dtype, down = {"e4m3": (ml_dtypes.float8_e4m3fn, 7), "e5m2": (ml_dtypes.float8_e5m2, 14)}[fmt]
    v = np.moveaxis(np.asarray(x, np.float32).astype(ml_dtypes.bfloat16).astype(np.float64), axis, -1)
    blocks = v.reshape(v.shape[:-1] + (-1, 32))
    amax = np.abs(blocks).max(-1, keepdims=True)
    byte = np.maximum(np.where(amax > 0, np.frexp(amax)[1] - 1 + 127, 0) - down, 1)
    scale = np.exp2(byte - 127.0)
    codes = (blocks / scale).astype(np.float32).astype(dtype).astype(np.float64)
    return np.moveaxis((codes * scale).reshape(v.shape), -1, axis)


WIDE = False


def mx_kscale(k):
    if not WIDE:
        return np.ones(k)
    levels = np.array([10, -10, 5, -5, 0])
    if k % 512:
        return np.exp2(np.random.permutation(np.resize(levels, k // 32))).repeat(32)
    a = np.empty((k // 512, 16))
    for p in range(k // 512):
        a[p, :8] = np.random.permutation(np.resize(levels, 8))
        for g in range(8):
            far = levels[np.abs(levels - a[p, g]) >= 10]
            a[p, g + 8] = far[np.random.randint(len(far))]
    return np.exp2(a.ravel()).repeat(32)


def f64(x):
    return np.asarray(x).astype(np.float64)


def striped(idx):
    return np.tile(idx.reshape(-1, 16).T, (8, 1)).astype(np.uint16)


def unstriped(offs):
    return offs[:16].T.reshape(-1).astype(np.int64)


def striped8(idx):
    return np.concatenate([x.reshape(-1, 16).T for x in idx]).astype(np.uint16)


def runs(offs, k):
    lists = np.stack([offs[16 * r : 16 * r + 16].T.reshape(-1) for r in range(8)]).astype(np.int64)
    return lists[np.arange(k) % 512 // 64]


def pack_weight(w):
    k, n = w.shape
    w = f64(np.asarray(w, np.float32).astype(ml_dtypes.bfloat16)).reshape(k // 32, 32, n)
    amax = np.abs(w).max(1)
    byte = np.clip(np.where(amax > 0, np.frexp(amax)[1] - 1 + 127 - 7, 1), 1, 254)
    scaled = (w * np.exp2(127.0 - byte)[:, None, :]).reshape(k, n).astype(np.float32)
    words = np.ascontiguousarray(scaled.reshape(k // 512, 128, 4, n).transpose(0, 1, 3, 2)).astype(ml_dtypes.float8_e4m3fn).view(np.uint8)
    return words, np.ascontiguousarray(byte.astype(np.uint8).reshape(k // 512, 16, n))


def unpack_weight(words, scales):
    g, p, n, _ = words.shape
    vals = np.ascontiguousarray(words).view(ml_dtypes.float8_e4m3fn).astype(np.float64) * np.repeat(np.exp2(scales.astype(np.float64) - 127.0), 8, axis=1)[..., None]
    return vals.transpose(0, 1, 3, 2).reshape(g * 512, n)

def planes(y):
    n, m = y.shape
    v = y.astype(np.float32).astype(ml_dtypes.bfloat16).astype(np.float64).reshape(n // 32, 32, m)
    top = np.abs(v).max(1)
    byte = np.clip(np.where(top > 0, np.frexp(top)[1] - 1 + 127 - 7, 1), 1, 254)
    codes = (v * np.exp2(127.0 - byte)[:, None, :]).reshape(n, m).astype(np.float32).astype(ml_dtypes.float8_e4m3fn).view(np.uint8)
    words = codes.reshape(n // 512, 128, 4, m).transpose(0, 1, 3, 2)
    return np.ascontiguousarray(words), np.ascontiguousarray(byte.astype(np.uint8).reshape(n // 512, 16, m))


K, T, S, N, G, H = 512, 2048, 256, 512, 2048, 512


def setup_inputs():
    n = np.random.standard_normal
    s = mx_kscale(K)[:, None]
    u = mx_kscale(K)
    packed_xT = pack_weight(n((K, T)) * s)
    packed_dT = pack_weight(n((K, G)) / s)
    packed_w1 = pack_weight(n((H, N)) / np.sqrt(2 * H) / u[:, None])
    packed_w2 = pack_weight(n((K, N)) / np.sqrt(2 * K) / s)
    return {
        "x_words": packed_xT[0],
        "x_scales": packed_xT[1],
        "d_words": packed_dT[0],
        "d_scales": packed_dT[1],
        "gn": (np.random.uniform(0.5, 1.5, (H, 1)) * u[:, None]).astype(np.float32),
        "w1_words": packed_w1[0],
        "w1_scales": packed_w1[1],
        "w2_words": packed_w2[0],
        "w2_scales": packed_w2[1],
        "tau": np.random.uniform(0.5, 1.2, (N, 1)).astype(np.float32),
        "offs": striped(np.random.permutation(T)[:S]),
        "k1": striped8(np.random.randint(0, G, (8, H))),
        "n1": striped(np.random.permutation(S)),
        "n2": striped(np.random.permutation(S)),
        "two": striped(np.random.permutation(T)[:S]),
        "n3": striped(np.random.permutation(S)),
        "n4": striped(np.random.permutation(S)),
    }


def reference(x_words, x_scales, d_words, d_scales, gn, w1_words, w1_scales, w2_words, w2_scales, tau, offs, k1, n1, n2, two, n3, n4):
    d_k1 = unpack_weight(d_words, d_scales)[np.arange(K)[:, None], runs(k1, K)]
    xq = unpack_weight(x_words, x_scales)[:, unstriped(offs)]
    s = 0.0625 * (d_k1.T @ xq)
    st = s - s[:, unstriped(n1)]
    z = f64(gn) * (st / (np.abs(st[:, unstriped(n2)]) + 0.5))
    x_two = unpack_weight(x_words, x_scales)[:, unstriped(two)]
    h = unpack_weight(w1_words, w1_scales).T @ mxq(z, 0, "e4m3") + unpack_weight(w2_words, w2_scales).T @ x_two
    sz = np.abs(h)
    ea = np.exp(-1.0 * (f64(tau) * sz[:, unstriped(n3)]))
    out_0 = (h - h[:, unstriped(n4)]) * ea
    return (out_0,) + planes(out_0)

@@ -1,0 +1,217 @@
+from contextlib import ExitStack
+
+import concourse.mybir as mybir
+
+K, T, S, N, G, H = 512, 2048, 256, 512, 2048, 512
+FLOPS = 2 * K * H * S + 2 * H * N * S + 2 * K * N * S
+
+F32 = mybir.dt.float32
+BF16 = mybir.dt.bfloat16
+I32 = mybir.dt.int32
+U32 = mybir.dt.uint32
+U16 = mybir.dt.uint16
+U8 = mybir.dt.uint8
+FP8X4 = mybir.dt.float8_e4m3fn_x4
+ALU = mybir.AluOpType
+ACT = mybir.ActivationFunctionType
+
+P = 128
+PACK = 4
+QUADRANTS = 4
+W2_ROW = 4
+NARROW = S + 16
+MIDDLE = S + 96
+WIDE = 2 * S
+
+
+def as_words(packed):
+    return packed[0].rearrange("p n t -> p (n t)").bitcast(I32)
+
+
+def tile_picked_kmixhopnela_none_po_kernel(
+    tc, x_words, x_scales, d_words, d_scales, gn, w1_words, w1_scales, w2_words, w2_scales, tau,
+    offs, k1, n1, n2, two, n3, n4, out_0, out_1, out_2,
+):
+    nc = tc.nc
+    with ExitStack() as ctx:
+        lists = ctx.enter_context(tc.tile_pool(name="lists", bufs=1))
+        sb = ctx.enter_context(tc.tile_pool(name="sb", bufs=1))
+        psum = ctx.enter_context(tc.psum_pool(name="psum", bufs=1))
+
+        def load_list(src, name):
+            tile = lists.tile(list(src.shape), U16, name=name)
+            nc.sync.dma_start(tile[:], src)
+            return tile
+
+        def mx_tile(width, dtype, name, tag=""):
+            return sb.tile([P, width], dtype, name=name, tag=tag, align_bytes=64)
+
+        d_scale_table = mx_tile(G, U8, "d_scale_table")
+        x_scale_table = mx_tile(T, U8, "x_scale_table", tag="tau_after")
+        nc.vector.memset(d_scale_table[:].bitcast(I32), 0)
+        nc.gpsimd.memset(x_scale_table[:].bitcast(I32), 0)
+        k1_list = load_list(k1, "k1_list")
+        offs_list = load_list(offs, "offs_list")
+        for c in range(2):
+            nc.sync.dma_start(d_scale_table[:].bitcast(I32)[c:P:16, :], d_scales[0].bitcast(I32)[c:16:2, :])
+        d_table = mx_tile(G, U32, "d_table", tag="word_rows")
+        nc.sync.dma_start(d_table[:].bitcast(I32), as_words(d_words))
+        for q in range(QUADRANTS):
+            nc.sync.dma_start(
+                x_scale_table[:].bitcast(I32)[32 * q : 32 * q + 4, :], x_scales[0].bitcast(I32)[4 * q : 4 * q + 4, :]
+            )
+        x_table = mx_tile(T, U32, "x_table")
+        nc.sync.dma_start(x_table[:].bitcast(I32), as_words(x_words))
+        two_list = load_list(two, "two_list")
+        n1_list = load_list(n1, "n1_list")
+        n2_list = load_list(n2, "n2_list")
+        n3_list = load_list(n3, "n3_list")
+        n4_list = load_list(n4, "n4_list")
+
+        key_scales_picked = mx_tile(H, U8, "key_scales_picked")
+        nc.vector.tensor_copy(key_scales_picked[:], d_scale_table[:].indirect(k1_list[:]))
+        key_scales_dealt = mx_tile(H, U8, "key_scales_dealt", tag="scale_rows")
+        nc.vector.tensor_copy(
+            key_scales_dealt[:].rearrange("p (t m) -> p m t", t=PACK),
+            key_scales_picked[:].rearrange("p (m t) -> p m t", t=PACK),
+        )
+        key_scales = mx_tile(H, U8, "key_scales")
+        nc.vector.tensor_copy(key_scales[:].bitcast(I32), key_scales_dealt[:].bitcast(I32))
+        for c in range(2):
+            nc.scalar.dma_start(
+                key_scales[:].bitcast(I32)[2 + c : P : 32, :],
+                key_scales_dealt[:].bitcast(I32)[16 + c : P : 32, :],
+            )
+
+        w_scale_rows = mx_tile(N, U8, "w_scale_rows", tag="scale_rows")
+        nc.vector.memset(w_scale_rows[:].bitcast(I32), 0)
+        for first_row, src in ((W2_ROW, w2_scales), (0, w1_scales)):
+            for q in range(QUADRANTS):
+                row = 32 * q + first_row
+                nc.sync.dma_start(
+                    w_scale_rows[:].bitcast(I32)[row : row + 4, :], src[0].bitcast(I32)[4 * q : 4 * q + 4, :]
+                )
+
+        key_words_picked = mx_tile(H, U32, "key_words_picked", tag="gn_after")
+        nc.vector.tensor_copy(key_words_picked[:], d_table[:].indirect(k1_list[:]))
+        key_words = mx_tile(H, U32, "key_words")
+        nc.vector.tensor_copy(
+            key_words[:].rearrange("p (t m) -> p m t", t=PACK),
+            key_words_picked[:].rearrange("p (m t) -> p m t", t=PACK),
+        )
+        w_word_rows = mx_tile(2 * N, U32, "w_word_rows", tag="word_rows")
+        nc.sync.dma_start(w_word_rows[:, N : 2 * N].bitcast(I32), as_words(w2_words))
+        nc.sync.dma_start(w_word_rows[:, 0:N].bitcast(I32), as_words(w1_words))
+        gn_cols = mx_tile(PACK, F32, "gn_cols", tag="gn_after")
+        nc.sync.dma_start(gn_cols[:], gn.rearrange("(p t) o -> p (t o)", t=PACK))
+        xq_scales = mx_tile(S, U8, "xq_scales")
+        nc.vector.tensor_copy(xq_scales[:], x_scale_table[:].indirect(offs_list[:]))
+        xq_words = mx_tile(S, U32, "xq_words")
+        nc.vector.tensor_copy(xq_words[:], x_table[:].indirect(offs_list[:]))
+        x2_scales = mx_tile(S, U8, "x2_scales")
+        nc.vector.tensor_copy(x2_scales[:], x_scale_table[:].indirect(two_list[:]))
+        tau_cols = mx_tile(PACK, F32, "tau_cols", tag="tau_after")
+        nc.sync.dma_start(tau_cols[:], tau.rearrange("(p t) o -> p (t o)", t=PACK))
+
+        s_banks = [psum.tile([P, S], F32, name=f"s_bank{t}") for t in range(PACK)]
+        h_banks = [psum.tile([P, S], F32, name=f"h_bank{t}") for t in range(PACK)]
+        for t in range(PACK):
+            cols = slice(P * t, P * (t + 1))
+            nc.tensor.matmul_mx(
+                out=s_banks[t][:], lhsT=key_words[:, cols].bitcast(FP8X4), lhsT_scale=key_scales[:, cols],
+                rhs=xq_words[:].bitcast(FP8X4), rhs_scale=xq_scales[:], start=True, stop=True,
+            )
+
+        def planes(name, width=S):
+            return [sb.tile([P, width], F32, name=f"{name}{t}") for t in range(PACK)]
+
+        s_win = [sb.tile([P, MIDDLE if t % 2 == 0 else NARROW], F32, name=f"s_win{t}") for t in range(PACK)]
+        for tile in s_win:
+            nc.gpsimd.memset(tile[:, S:], 0.0)
+        r_win, h_win, sz_win = planes("r_win", WIDE), planes("h_win", WIDE), planes("sz_win", WIDE)
+        s_far = planes("s_far")
+        st = [tile[:, S:WIDE] for tile in sz_win]
+        st_size = [tile[:, S:WIDE] for tile in h_win]
+        root = [tile[:, S:WIDE] for tile in r_win]
+        z = sb.tile([P, PACK, S], F32, name="z")
+        x2_words = mx_tile(S, U32, "x2_words")
+        nc.vector.tensor_copy(x2_words[:], x_table[:].indirect(two_list[:]))
+        for t in range(PACK):
+            nc.scalar.activation(s_win[t][:, 0:S], s_banks[t][:], ACT.Copy, scale=0.0625)
+            if t % 2 == 0:
+                nc.vector.tensor_copy(s_far[t][:], s_win[t][:].indirect(n1_list[:]))
+            else:
+                nc.scalar.activation(s_far[t][:], s_win[t][:].indirect(n1_list[:]), ACT.Copy)
+            nc.vector.scalar_tensor_tensor(st[t], s_banks[t][:], 0.0625, s_far[t][:], ALU.mult, ALU.subtract)
+            nc.scalar.activation(st_size[t], st[t], ACT.Abs)
+            nc.scalar.activation(root[t], st_size[t], ACT.Abs_reciprocal_sqrt, bias=0.5)
+            gain = gn_cols[:, t : t + 1]
+            if t < PACK - 1:
+                nc.vector.scalar_tensor_tensor(r_win[t][:, 0:S], root[t], gain, root[t], ALU.mult, ALU.mult)
+                nc.vector.tensor_tensor(z[:, t, :], r_win[t][:].indirect(n2_list[:]), st[t], ALU.mult)
+            else:
+                r_far = sb.tile([P, S], F32, name="r_far")
+                nc.scalar.activation(r_win[t][:, 0:S], root[t], ACT.Square)
+                nc.scalar.activation(r_far[:], r_win[t][:].indirect(n2_list[:]), ACT.Copy)
+                nc.vector.scalar_tensor_tensor(z[:, t, :], r_far[:], gain, st[t], ALU.mult, ALU.mult)
+
+        w_words = mx_tile(2 * N, U32, "w_words")
+        for cols in (slice(N, 2 * N), slice(0, N)):
+            nc.gpsimd.tensor_copy(
+                w_words[:, cols].rearrange("p (t m) -> p t m", t=PACK),
+                w_word_rows[:, cols].rearrange("p (m t) -> p t m", t=PACK),
+            )
+        w_scales = mx_tile(N, U8, "w_scales")
+        nc.gpsimd.tensor_copy(
+            w_scales[:].rearrange("p (t m) -> p t m", t=PACK),
+            w_scale_rows[:].rearrange("p (m t) -> p t m", t=PACK),
+        )
+        minus_tau = sb.tile([P, PACK], F32, name="minus_tau")
+        nc.vector.tensor_scalar(minus_tau[:], tau_cols[:], -1.0, None, ALU.mult)
+        for t in range(PACK):
+            nc.tensor.matmul_mx(
+                out=h_banks[t][:], lhsT=w_words[:, N + P * t : N + P * (t + 1)].bitcast(FP8X4),
+                lhsT_scale=w_scales[W2_ROW:P, P * t : P * (t + 1)],
+                rhs=x2_words[:].bitcast(FP8X4), rhs_scale=x2_scales[:], start=True, stop=False,
+            )
+
+        def quantize(values, name):
+            rounded = sb.tile([P, S, PACK], BF16, name=f"{name}_rounded", align_bytes=64)
+            nc.vector.tensor_copy(
+                rounded[:].rearrange("p (c i) t -> p c t i", i=4), values[:].rearrange("p t (c i) -> p c t i", i=4)
+            )
+            words = mx_tile(S, U32, f"{name}_words")
+            scales = mx_tile(S, U8, f"{name}_scales")
+            nc.vector.quantize_mx(
+                out=words[:].bitcast(FP8X4), scales=scales[:], in_=rounded[:].rearrange("p j t -> p (j t)")
+            )
+            return words, scales
+
+        z_words, z_scales = quantize(z, "z")
+        for t in range(PACK):
+            cols = slice(P * t, P * (t + 1))
+            nc.tensor.matmul_mx(
+                out=h_banks[t][:], lhsT=w_words[:, cols].bitcast(FP8X4), lhsT_scale=w_scales[:, cols],
+                rhs=z_words[:].bitcast(FP8X4), rhs_scale=z_scales[:], start=False, stop=True,
+            )
+
+        h_far, h_diff, ea = planes("h_far"), planes("h_diff"), planes("ea")
+        y = sb.tile([P, PACK, S], F32, name="y")
+        out_rows = out_0.rearrange("(p t) j -> p t j", t=PACK)
+        for t in range(PACK):
+            if t == 0:
+                nc.vector.tensor_copy(h_win[t][:, 0:S], h_banks[t][:])
+            else:
+                nc.scalar.activation(h_win[t][:, 0:S], h_banks[t][:], ACT.Copy)
+            nc.scalar.activation(sz_win[t][:, 0:S], h_banks[t][:], ACT.Abs)
+            nc.scalar.activation(ea[t][:], sz_win[t][:].indirect(n3_list[:]), ACT.Exp, scale=minus_tau[:, t : t + 1])
+            nc.vector.tensor_copy(h_far[t][:], h_win[t][:].indirect(n4_list[:]))
+            nc.vector.tensor_tensor(h_diff[t][:], h_banks[t][:], h_far[t][:], ALU.subtract)
+            nc.vector.tensor_tensor(y[:, t, :], h_diff[t][:], ea[t][:], ALU.mult)
+            nc.sync.dma_start(out_rows[:, t, :], y[:, t, :])
+
+        y_words, y_scales = quantize(y, "y")
+        nc.sync.dma_start(as_words(out_1), y_words[:].bitcast(I32))
+        for q in range(QUADRANTS):
+            queue = nc.scalar if q % 2 == 0 else nc.sync
+            queue.dma_start(out_2[0].bitcast(I32)[4 * q : 4 * q + 4, :], y_scales[:].bitcast(I32)[32 * q : 32 * q + 4, :])

@@ -128,6 +128,10 @@ def tile_picked_kmixhopnela_none_po_kernel(
         s_win = [sb.tile([P, MIDDLE if t % 2 == 0 else NARROW], F32, name=f"s_win{t}") for t in range(PACK)]
         for tile in s_win:
             nc.gpsimd.memset(tile[:, S:], 0.0)
+        warm_in = sb.tile([P, 1], F32, name="warm_in")
+        warm_out = sb.tile([P, 2], F32, name="warm_out")
+        nc.gpsimd.memset(warm_in[:], 1.0)
+        nc.scalar.activation(warm_out[:, 0:1], warm_in[:], ACT.Abs_reciprocal_sqrt)
         r_win, h_win, sz_win = planes("r_win", WIDE), planes("h_win", WIDE), planes("sz_win", WIDE)
         s_far = planes("s_far")
         st = [tile[:, S:WIDE] for tile in sz_win]
@@ -174,6 +178,7 @@ def tile_picked_kmixhopnela_none_po_kernel(
                 lhsT_scale=w_scales[W2_ROW:P, P * t : P * (t + 1)],
                 rhs=x2_words[:].bitcast(FP8X4), rhs_scale=x2_scales[:], start=True, stop=False,
             )
+        nc.scalar.activation(warm_out[:, 1:2], r_far[:, 0:1], ACT.Exp)
 
         def quantize(values, name):
             rounded = sb.tile([P, S, PACK], BF16, name=f"{name}_rounded", align_bytes=64)

@@ -47,14 +47,14 @@ def tile_picked_kmixhopnela_none_po_kernel(
             return sb.tile([P, width], dtype, name=name, tag=tag, align_bytes=64)
 
         d_scale_table = mx_tile(G, U8, "d_scale_table")
-        x_scale_table = mx_tile(T, U8, "x_scale_table", tag="tau_after")
+        x_scale_table = mx_tile(T, U8, "x_scale_table")
         nc.vector.memset(d_scale_table[:].bitcast(I32), 0)
-        nc.gpsimd.memset(x_scale_table[:].bitcast(I32), 0)
+        nc.vector.memset(x_scale_table[:].bitcast(I32), 0)
         k1_list = load_list(k1, "k1_list")
         offs_list = load_list(offs, "offs_list")
         for c in range(2):
             nc.sync.dma_start(d_scale_table[:].bitcast(I32)[c:P:16, :], d_scales[0].bitcast(I32)[c:16:2, :])
-        d_table = mx_tile(G, U32, "d_table", tag="word_rows")
+        d_table = mx_tile(G, U32, "d_table")
         nc.sync.dma_start(d_table[:].bitcast(I32), as_words(d_words))
         for q in range(QUADRANTS):
             nc.sync.dma_start(
@@ -64,16 +64,31 @@ def tile_picked_kmixhopnela_none_po_kernel(
         nc.sync.dma_start(x_table[:].bitcast(I32), as_words(x_words))
         two_list = load_list(two, "two_list")
         n1_list = load_list(n1, "n1_list")
+        w_word_rows = mx_tile(2 * N, U32, "w_word_rows")
+        nc.sync.dma_start(w_word_rows[:, N : 2 * N].bitcast(I32), as_words(w2_words))
+        nc.sync.dma_start(w_word_rows[:, 0:N].bitcast(I32), as_words(w1_words))
         n2_list = load_list(n2, "n2_list")
+        gn_cols = mx_tile(PACK, F32, "gn_cols")
+        nc.sync.dma_start(gn_cols[:], gn.rearrange("(p t) o -> p (t o)", t=PACK))
+        w_scale_rows = mx_tile(N, U8, "w_scale_rows")
+        nc.vector.memset(w_scale_rows[:].bitcast(I32), 0)
+        for first_row, src in ((W2_ROW, w2_scales), (0, w1_scales)):
+            for q in range(QUADRANTS):
+                row = 32 * q + first_row
+                nc.sync.dma_start(
+                    w_scale_rows[:].bitcast(I32)[row : row + 4, :], src[0].bitcast(I32)[4 * q : 4 * q + 4, :]
+                )
+        tau_cols = mx_tile(PACK, F32, "tau_cols")
+        nc.sync.dma_start(tau_cols[:], tau.rearrange("(p t) o -> p (t o)", t=PACK))
         n3_list = load_list(n3, "n3_list")
         n4_list = load_list(n4, "n4_list")
 
         key_scales_picked = mx_tile(H, U8, "key_scales_picked")
         nc.vector.tensor_copy(key_scales_picked[:], d_scale_table[:].indirect(k1_list[:]))
-        key_scales_dealt = mx_tile(H, U8, "key_scales_dealt", tag="scale_rows")
+        key_scales_dealt = mx_tile(H, U8, "key_scales_dealt")
         nc.vector.tensor_copy(
-            key_scales_dealt[:].rearrange("p (t m) -> p m t", t=PACK),
-            key_scales_picked[:].rearrange("p (m t) -> p m t", t=PACK),
+            key_scales_dealt[:].rearrange("p (t m) -> p t m", t=PACK),
+            key_scales_picked[:].rearrange("p (m t) -> p t m", t=PACK),
         )
         key_scales = mx_tile(H, U8, "key_scales")
         nc.vector.tensor_copy(key_scales[:].bitcast(I32), key_scales_dealt[:].bitcast(I32))
@@ -83,35 +98,19 @@ def tile_picked_kmixhopnela_none_po_kernel(
                 key_scales_dealt[:].bitcast(I32)[16 + c : P : 32, :],
             )
 
-        w_scale_rows = mx_tile(N, U8, "w_scale_rows", tag="scale_rows")
-        nc.vector.memset(w_scale_rows[:].bitcast(I32), 0)
-        for first_row, src in ((W2_ROW, w2_scales), (0, w1_scales)):
-            for q in range(QUADRANTS):
-                row = 32 * q + first_row
-                nc.sync.dma_start(
-                    w_scale_rows[:].bitcast(I32)[row : row + 4, :], src[0].bitcast(I32)[4 * q : 4 * q + 4, :]
-                )
-
-        key_words_picked = mx_tile(H, U32, "key_words_picked", tag="gn_after")
+        key_words_picked = mx_tile(H, U32, "key_words_picked")
         nc.vector.tensor_copy(key_words_picked[:], d_table[:].indirect(k1_list[:]))
         key_words = mx_tile(H, U32, "key_words")
         nc.vector.tensor_copy(
             key_words[:].rearrange("p (t m) -> p m t", t=PACK),
             key_words_picked[:].rearrange("p (m t) -> p m t", t=PACK),
         )
-        w_word_rows = mx_tile(2 * N, U32, "w_word_rows", tag="word_rows")
-        nc.sync.dma_start(w_word_rows[:, N : 2 * N].bitcast(I32), as_words(w2_words))
-        nc.sync.dma_start(w_word_rows[:, 0:N].bitcast(I32), as_words(w1_words))
-        gn_cols = mx_tile(PACK, F32, "gn_cols", tag="gn_after")
-        nc.sync.dma_start(gn_cols[:], gn.rearrange("(p t) o -> p (t o)", t=PACK))
         xq_scales = mx_tile(S, U8, "xq_scales")
         nc.vector.tensor_copy(xq_scales[:], x_scale_table[:].indirect(offs_list[:]))
         xq_words = mx_tile(S, U32, "xq_words")
         nc.vector.tensor_copy(xq_words[:], x_table[:].indirect(offs_list[:]))
         x2_scales = mx_tile(S, U8, "x2_scales")
         nc.vector.tensor_copy(x2_scales[:], x_scale_table[:].indirect(two_list[:]))
-        tau_cols = mx_tile(PACK, F32, "tau_cols", tag="tau_after")
-        nc.sync.dma_start(tau_cols[:], tau.rearrange("(p t) o -> p (t o)", t=PACK))
 
         s_banks = [psum.tile([P, S], F32, name=f"s_bank{t}") for t in range(PACK)]
         h_banks = [psum.tile([P, S], F32, name=f"h_bank{t}") for t in range(PACK)]
@@ -125,24 +124,28 @@ def tile_picked_kmixhopnela_none_po_kernel(
         def planes(name, width=S):
             return [sb.tile([P, width], F32, name=f"{name}{t}") for t in range(PACK)]
 
-        s_win = [sb.tile([P, MIDDLE if t % 2 == 0 else NARROW], F32, name=f"s_win{t}") for t in range(PACK)]
+        s_win = [sb.tile([P, MIDDLE if t % 2 == 1 else NARROW], F32, name=f"s_win{t}") for t in range(PACK)]
         for tile in s_win:
-            nc.gpsimd.memset(tile[:, S:], 0.0)
+            nc.vector.memset(tile[:, S:], 0.0)
         warm_in = sb.tile([P, 1], F32, name="warm_in")
         warm_out = sb.tile([P, 2], F32, name="warm_out")
-        nc.gpsimd.memset(warm_in[:], 1.0)
+        nc.vector.memset(warm_in[:], 1.0)
         nc.scalar.activation(warm_out[:, 0:1], warm_in[:], ACT.Abs_reciprocal_sqrt)
         r_win, h_win, sz_win = planes("r_win", WIDE), planes("h_win", WIDE), planes("sz_win", WIDE)
         s_far = planes("s_far")
         st = [tile[:, S:WIDE] for tile in sz_win]
         st_size = [tile[:, S:WIDE] for tile in h_win]
         root = [tile[:, S:WIDE] for tile in r_win]
+        halves = (slice(0, S // 2), slice(S // 2, S))
         z = sb.tile([P, PACK, S], F32, name="z")
         x2_words = mx_tile(S, U32, "x2_words")
         nc.vector.tensor_copy(x2_words[:], x_table[:].indirect(two_list[:]))
         for t in range(PACK):
-            nc.scalar.activation(s_win[t][:, 0:S], s_banks[t][:], ACT.Copy, scale=0.0625)
-            if t % 2 == 0:
+            if t == 1:
+                nc.vector.tensor_scalar(s_win[t][:, 0:S], s_banks[t][:], 0.0625, None, ALU.mult)
+            else:
+                nc.scalar.activation(s_win[t][:, 0:S], s_banks[t][:], ACT.Copy, scale=0.0625)
+            if t % 2 == 1:
                 nc.vector.tensor_copy(s_far[t][:], s_win[t][:].indirect(n1_list[:]))
             else:
                 nc.scalar.activation(s_far[t][:], s_win[t][:].indirect(n1_list[:]), ACT.Copy)
@@ -157,7 +160,8 @@ def tile_picked_kmixhopnela_none_po_kernel(
                 r_far = sb.tile([P, S], F32, name="r_far")
                 nc.scalar.activation(r_win[t][:, 0:S], root[t], ACT.Square)
                 nc.scalar.activation(r_far[:], r_win[t][:].indirect(n2_list[:]), ACT.Copy)
-                nc.vector.scalar_tensor_tensor(z[:, t, :], r_far[:], gain, st[t], ALU.mult, ALU.mult)
+                for cols in halves:
+                    nc.vector.scalar_tensor_tensor(z[:, t, cols], r_far[:, cols], gain, st[t][:, cols], ALU.mult, ALU.mult)
 
         w_words = mx_tile(2 * N, U32, "w_words")
         for cols in (slice(N, 2 * N), slice(0, N)):
@@ -180,42 +184,71 @@ def tile_picked_kmixhopnela_none_po_kernel(
             )
         nc.scalar.activation(warm_out[:, 1:2], r_far[:, 0:1], ACT.Exp)
 
-        def quantize(values, name):
-            rounded = sb.tile([P, S, PACK], BF16, name=f"{name}_rounded", align_bytes=64)
-            nc.vector.tensor_copy(
-                rounded[:].rearrange("p (c i) t -> p c t i", i=4), values[:].rearrange("p t (c i) -> p c t i", i=4)
+        def interleave(engine_copy, rounded, values, cols):
+            engine_copy(
+                rounded[:, cols, :].rearrange("p (c i) t -> p c t i", i=4),
+                values[:, :, cols].rearrange("p t (c i) -> p c t i", i=4),
             )
-            words = mx_tile(S, U32, f"{name}_words")
-            scales = mx_tile(S, U8, f"{name}_scales")
-            nc.vector.quantize_mx(
-                out=words[:].bitcast(FP8X4), scales=scales[:], in_=rounded[:].rearrange("p j t -> p (j t)")
-            )
-            return words, scales
 
-        z_words, z_scales = quantize(z, "z")
-        for t in range(PACK):
-            cols = slice(P * t, P * (t + 1))
-            nc.tensor.matmul_mx(
-                out=h_banks[t][:], lhsT=w_words[:, cols].bitcast(FP8X4), lhsT_scale=w_scales[:, cols],
-                rhs=z_words[:].bitcast(FP8X4), rhs_scale=z_scales[:], start=False, stop=True,
+        def quantize(words, scales, rounded, cols):
+            nc.vector.quantize_mx(
+                out=words[:, cols].bitcast(FP8X4), scales=scales[:, cols],
+                in_=rounded[:, cols, :].rearrange("p j t -> p (j t)"),
             )
+
+        z_rounded = sb.tile([P, S, PACK], BF16, name="z_rounded", align_bytes=64)
+        z_words, z_scales = mx_tile(S, U32, "z_words"), mx_tile(S, U8, "z_scales")
+        for cols in halves:
+            interleave(nc.vector.tensor_copy, z_rounded, z, cols)
+        for cols in halves:
+            quantize(z_words, z_scales, z_rounded, cols)
+        for cols in halves:
+            for t in range(PACK):
+                rows = slice(P * t, P * (t + 1))
+                nc.tensor.matmul_mx(
+                    out=h_banks[t][:, cols], lhsT=w_words[:, rows].bitcast(FP8X4), lhsT_scale=w_scales[:, rows],
+                    rhs=z_words[:, cols].bitcast(FP8X4), rhs_scale=z_scales[:, cols],
+                    start=False, stop=(cols == halves[1]),
+                )
 
         h_far, h_diff, ea = planes("h_far"), planes("h_diff"), planes("ea")
         y = sb.tile([P, PACK, S], F32, name="y")
         out_rows = out_0.rearrange("(p t) j -> p t j", t=PACK)
-        for t in range(PACK):
-            if t == 0:
+
+        def copy_out(t):
+            if t == 2:
                 nc.vector.tensor_copy(h_win[t][:, 0:S], h_banks[t][:])
             else:
                 nc.scalar.activation(h_win[t][:, 0:S], h_banks[t][:], ACT.Copy)
-            nc.scalar.activation(sz_win[t][:, 0:S], h_banks[t][:], ACT.Abs)
-            nc.scalar.activation(ea[t][:], sz_win[t][:].indirect(n3_list[:]), ACT.Exp, scale=minus_tau[:, t : t + 1])
+
+        def fetch(t):
             nc.vector.tensor_copy(h_far[t][:], h_win[t][:].indirect(n4_list[:]))
+
+        def size(t):
+            nc.scalar.activation(sz_win[t][:, 0:S], h_banks[t][:], ACT.Abs)
+
+        def decay(t):
+            nc.scalar.activation(ea[t][:], sz_win[t][:].indirect(n3_list[:]), ACT.Exp, scale=minus_tau[:, t : t + 1])
+
+        def differ(t):
             nc.vector.tensor_tensor(h_diff[t][:], h_banks[t][:], h_far[t][:], ALU.subtract)
-            nc.vector.tensor_tensor(y[:, t, :], h_diff[t][:], ea[t][:], ALU.mult)
+
+        def finish(t):
+            engine = nc.gpsimd if t < 2 else nc.vector
+            engine.tensor_tensor(y[:, t, :], h_diff[t][:], ea[t][:], ALU.mult)
             nc.sync.dma_start(out_rows[:, t, :], y[:, t, :])
 
-        y_words, y_scales = quantize(y, "y")
+        steps = (copy_out, fetch, size, decay, differ, finish)
+        for wave in range(len(steps) + PACK - 1):
+            for t in range(PACK):
+                if 0 <= wave - t < len(steps):
+                    steps[wave - t](t)
+
+        y_rounded = sb.tile([P, S, PACK], BF16, name="y_rounded", align_bytes=64)
+        y_words, y_scales = mx_tile(S, U32, "y_words"), mx_tile(S, U8, "y_scales")
+        interleave(nc.scalar.copy, y_rounded, y, slice(0, 80))
+        interleave(nc.vector.tensor_copy, y_rounded, y, slice(80, S))
+        quantize(y_words, y_scales, y_rounded, slice(0, S))
         nc.sync.dma_start(as_words(out_1), y_words[:].bitcast(I32))
         for q in range(QUADRANTS):
             queue = nc.scalar if q % 2 == 0 else nc.sync

@@ -19,9 +19,16 @@ P = 128
 PACK = 4
 QUADRANTS = 4
 W2_ROW = 4
-NARROW = S + 16
-MIDDLE = S + 96
+S_SCALE = 0.0625
+
+SCALAR_WINDOW = S + 16
+VECTOR_WINDOW = S + 96
 WIDE = 2 * S
+
+S_COPY_ON_VECTOR = 1
+H_COPY_ON_VECTOR = 2
+GPSIMD_PRODUCTS = 2
+SCALAR_ROUND_COLS = 80
 
 
 def as_words(packed):
@@ -43,8 +50,8 @@ def tile_picked_kmixhopnela_none_po_kernel(
             nc.sync.dma_start(tile[:], src)
             return tile
 
-        def mx_tile(width, dtype, name, tag=""):
-            return sb.tile([P, width], dtype, name=name, tag=tag, align_bytes=64)
+        def mx_tile(width, dtype, name):
+            return sb.tile([P, width], dtype, name=name, align_bytes=64)
 
         d_scale_table = mx_tile(G, U8, "d_scale_table")
         x_scale_table = mx_tile(T, U8, "x_scale_table")
@@ -115,22 +122,25 @@ def tile_picked_kmixhopnela_none_po_kernel(
         s_banks = [psum.tile([P, S], F32, name=f"s_bank{t}") for t in range(PACK)]
         h_banks = [psum.tile([P, S], F32, name=f"h_bank{t}") for t in range(PACK)]
         for t in range(PACK):
-            cols = slice(P * t, P * (t + 1))
+            rows = slice(P * t, P * (t + 1))
             nc.tensor.matmul_mx(
-                out=s_banks[t][:], lhsT=key_words[:, cols].bitcast(FP8X4), lhsT_scale=key_scales[:, cols],
+                out=s_banks[t][:], lhsT=key_words[:, rows].bitcast(FP8X4), lhsT_scale=key_scales[:, rows],
                 rhs=xq_words[:].bitcast(FP8X4), rhs_scale=xq_scales[:], start=True, stop=True,
             )
 
         def planes(name, width=S):
             return [sb.tile([P, width], F32, name=f"{name}{t}") for t in range(PACK)]
 
-        s_win = [sb.tile([P, MIDDLE if t % 2 == 1 else NARROW], F32, name=f"s_win{t}") for t in range(PACK)]
+        s_win = [
+            sb.tile([P, VECTOR_WINDOW if t % 2 == 1 else SCALAR_WINDOW], F32, name=f"s_win{t}") for t in range(PACK)
+        ]
         for tile in s_win:
             nc.vector.memset(tile[:, S:], 0.0)
         warm_in = sb.tile([P, 1], F32, name="warm_in")
         warm_out = sb.tile([P, 2], F32, name="warm_out")
         nc.vector.memset(warm_in[:], 1.0)
         nc.scalar.activation(warm_out[:, 0:1], warm_in[:], ACT.Abs_reciprocal_sqrt)
+
         r_win, h_win, sz_win = planes("r_win", WIDE), planes("h_win", WIDE), planes("sz_win", WIDE)
         s_far = planes("s_far")
         st = [tile[:, S:WIDE] for tile in sz_win]
@@ -140,16 +150,17 @@ def tile_picked_kmixhopnela_none_po_kernel(
         z = sb.tile([P, PACK, S], F32, name="z")
         x2_words = mx_tile(S, U32, "x2_words")
         nc.vector.tensor_copy(x2_words[:], x_table[:].indirect(two_list[:]))
+
         for t in range(PACK):
-            if t == 1:
-                nc.vector.tensor_scalar(s_win[t][:, 0:S], s_banks[t][:], 0.0625, None, ALU.mult)
+            if t == S_COPY_ON_VECTOR:
+                nc.vector.tensor_scalar(s_win[t][:, 0:S], s_banks[t][:], S_SCALE, None, ALU.mult)
             else:
-                nc.scalar.activation(s_win[t][:, 0:S], s_banks[t][:], ACT.Copy, scale=0.0625)
+                nc.scalar.activation(s_win[t][:, 0:S], s_banks[t][:], ACT.Copy, scale=S_SCALE)
             if t % 2 == 1:
                 nc.vector.tensor_copy(s_far[t][:], s_win[t][:].indirect(n1_list[:]))
             else:
                 nc.scalar.activation(s_far[t][:], s_win[t][:].indirect(n1_list[:]), ACT.Copy)
-            nc.vector.scalar_tensor_tensor(st[t], s_banks[t][:], 0.0625, s_far[t][:], ALU.mult, ALU.subtract)
+            nc.vector.scalar_tensor_tensor(st[t], s_banks[t][:], S_SCALE, s_far[t][:], ALU.mult, ALU.subtract)
             nc.scalar.activation(st_size[t], st[t], ACT.Abs)
             nc.scalar.activation(root[t], st_size[t], ACT.Abs_reciprocal_sqrt, bias=0.5)
             gain = gn_cols[:, t : t + 1]
@@ -161,13 +172,15 @@ def tile_picked_kmixhopnela_none_po_kernel(
                 nc.scalar.activation(r_win[t][:, 0:S], root[t], ACT.Square)
                 nc.scalar.activation(r_far[:], r_win[t][:].indirect(n2_list[:]), ACT.Copy)
                 for cols in halves:
-                    nc.vector.scalar_tensor_tensor(z[:, t, cols], r_far[:, cols], gain, st[t][:, cols], ALU.mult, ALU.mult)
+                    nc.vector.scalar_tensor_tensor(
+                        z[:, t, cols], r_far[:, cols], gain, st[t][:, cols], ALU.mult, ALU.mult
+                    )
 
         w_words = mx_tile(2 * N, U32, "w_words")
-        for cols in (slice(N, 2 * N), slice(0, N)):
+        for matrix in (slice(N, 2 * N), slice(0, N)):
             nc.gpsimd.tensor_copy(
-                w_words[:, cols].rearrange("p (t m) -> p t m", t=PACK),
-                w_word_rows[:, cols].rearrange("p (m t) -> p t m", t=PACK),
+                w_words[:, matrix].rearrange("p (t m) -> p t m", t=PACK),
+                w_word_rows[:, matrix].rearrange("p (m t) -> p t m", t=PACK),
             )
         w_scales = mx_tile(N, U8, "w_scales")
         nc.gpsimd.tensor_copy(
@@ -202,9 +215,9 @@ def tile_picked_kmixhopnela_none_po_kernel(
             interleave(nc.vector.tensor_copy, z_rounded, z, cols)
         for cols in halves:
             quantize(z_words, z_scales, z_rounded, cols)
-        for cols in halves:
-            for t in range(PACK):
-                rows = slice(P * t, P * (t + 1))
+        for t in range(PACK):
+            rows = slice(P * t, P * (t + 1))
+            for cols in halves:
                 nc.tensor.matmul_mx(
                     out=h_banks[t][:, cols], lhsT=w_words[:, rows].bitcast(FP8X4), lhsT_scale=w_scales[:, rows],
                     rhs=z_words[:, cols].bitcast(FP8X4), rhs_scale=z_scales[:, cols],
@@ -216,7 +229,7 @@ def tile_picked_kmixhopnela_none_po_kernel(
         out_rows = out_0.rearrange("(p t) j -> p t j", t=PACK)
 
         def copy_out(t):
-            if t == 2:
+            if t == H_COPY_ON_VECTOR:
                 nc.vector.tensor_copy(h_win[t][:, 0:S], h_banks[t][:])
             else:
                 nc.scalar.activation(h_win[t][:, 0:S], h_banks[t][:], ACT.Copy)
@@ -234,7 +247,7 @@ def tile_picked_kmixhopnela_none_po_kernel(
             nc.vector.tensor_tensor(h_diff[t][:], h_banks[t][:], h_far[t][:], ALU.subtract)
 
         def finish(t):
-            engine = nc.gpsimd if t < 2 else nc.vector
+            engine = nc.gpsimd if t < GPSIMD_PRODUCTS else nc.vector
             engine.tensor_tensor(y[:, t, :], h_diff[t][:], ea[t][:], ALU.mult)
             nc.sync.dma_start(out_rows[:, t, :], y[:, t, :])
 
@@ -246,10 +259,12 @@ def tile_picked_kmixhopnela_none_po_kernel(
 
         y_rounded = sb.tile([P, S, PACK], BF16, name="y_rounded", align_bytes=64)
         y_words, y_scales = mx_tile(S, U32, "y_words"), mx_tile(S, U8, "y_scales")
-        interleave(nc.scalar.copy, y_rounded, y, slice(0, 80))
-        interleave(nc.vector.tensor_copy, y_rounded, y, slice(80, S))
+        interleave(nc.scalar.copy, y_rounded, y, slice(0, SCALAR_ROUND_COLS))
+        interleave(nc.vector.tensor_copy, y_rounded, y, slice(SCALAR_ROUND_COLS, S))
         quantize(y_words, y_scales, y_rounded, slice(0, S))
         nc.sync.dma_start(as_words(out_1), y_words[:].bitcast(I32))
         for q in range(QUADRANTS):
             queue = nc.scalar if q % 2 == 0 else nc.sync
-            queue.dma_start(out_2[0].bitcast(I32)[4 * q : 4 * q + 4, :], y_scales[:].bitcast(I32)[32 * q : 32 * q + 4, :])
+            queue.dma_start(
+                out_2[0].bitcast(I32)[4 * q : 4 * q + 4, :], y_scales[:].bitcast(I32)[32 * q : 32 * q + 4, :]
+            )

from contextlib import ExitStack

import concourse.mybir as mybir

K, T, S, N, G, H = 512, 2048, 256, 512, 2048, 512
FLOPS = 2 * K * H * S + 2 * H * N * S + 2 * K * N * S

F32 = mybir.dt.float32
BF16 = mybir.dt.bfloat16
I32 = mybir.dt.int32
U32 = mybir.dt.uint32
U16 = mybir.dt.uint16
U8 = mybir.dt.uint8
FP8X4 = mybir.dt.float8_e4m3fn_x4
ALU = mybir.AluOpType
ACT = mybir.ActivationFunctionType

P = 128
PACK = 4
QUADRANTS = 4
W2_ROW = 4
S_SCALE = 0.0625

SCALAR_WINDOW = S + 16
VECTOR_WINDOW = S + 96
WIDE = 2 * S

S_COPY_ON_VECTOR = 1
H_COPY_ON_VECTOR = 2
GPSIMD_PRODUCTS = 2
SCALAR_ROUND_COLS = 80


def as_words(packed):
    return packed[0].rearrange("p n t -> p (n t)").bitcast(I32)


def tile_picked_kmixhopnela_none_po_kernel(
    tc, x_words, x_scales, d_words, d_scales, gn, w1_words, w1_scales, w2_words, w2_scales, tau,
    offs, k1, n1, n2, two, n3, n4, out_0, out_1, out_2,
):
    nc = tc.nc
    with ExitStack() as ctx:
        lists = ctx.enter_context(tc.tile_pool(name="lists", bufs=1))
        sb = ctx.enter_context(tc.tile_pool(name="sb", bufs=1))
        psum = ctx.enter_context(tc.psum_pool(name="psum", bufs=1))

        def load_list(src, name):
            tile = lists.tile(list(src.shape), U16, name=name)
            nc.sync.dma_start(tile[:], src)
            return tile

        def mx_tile(width, dtype, name):
            return sb.tile([P, width], dtype, name=name, align_bytes=64)

        d_scale_table = mx_tile(G, U8, "d_scale_table")
        x_scale_table = mx_tile(T, U8, "x_scale_table")
        nc.vector.memset(d_scale_table[:].bitcast(I32), 0)
        nc.vector.memset(x_scale_table[:].bitcast(I32), 0)
        k1_list = load_list(k1, "k1_list")
        offs_list = load_list(offs, "offs_list")
        for c in range(2):
            nc.sync.dma_start(d_scale_table[:].bitcast(I32)[c:P:16, :], d_scales[0].bitcast(I32)[c:16:2, :])
        d_table = mx_tile(G, U32, "d_table")
        nc.sync.dma_start(d_table[:].bitcast(I32), as_words(d_words))
        for q in range(QUADRANTS):
            nc.sync.dma_start(
                x_scale_table[:].bitcast(I32)[32 * q : 32 * q + 4, :], x_scales[0].bitcast(I32)[4 * q : 4 * q + 4, :]
            )
        x_table = mx_tile(T, U32, "x_table")
        nc.sync.dma_start(x_table[:].bitcast(I32), as_words(x_words))
        two_list = load_list(two, "two_list")
        n1_list = load_list(n1, "n1_list")
        w_word_rows = mx_tile(2 * N, U32, "w_word_rows")
        nc.sync.dma_start(w_word_rows[:, N : 2 * N].bitcast(I32), as_words(w2_words))
        nc.sync.dma_start(w_word_rows[:, 0:N].bitcast(I32), as_words(w1_words))
        n2_list = load_list(n2, "n2_list")
        gn_cols = mx_tile(PACK, F32, "gn_cols")
        nc.sync.dma_start(gn_cols[:], gn.rearrange("(p t) o -> p (t o)", t=PACK))
        w_scale_rows = mx_tile(N, U8, "w_scale_rows")
        nc.vector.memset(w_scale_rows[:].bitcast(I32), 0)
        for first_row, src in ((W2_ROW, w2_scales), (0, w1_scales)):
            for q in range(QUADRANTS):
                row = 32 * q + first_row
                nc.sync.dma_start(
                    w_scale_rows[:].bitcast(I32)[row : row + 4, :], src[0].bitcast(I32)[4 * q : 4 * q + 4, :]
                )
        tau_cols = mx_tile(PACK, F32, "tau_cols")
        nc.sync.dma_start(tau_cols[:], tau.rearrange("(p t) o -> p (t o)", t=PACK))
        n3_list = load_list(n3, "n3_list")
        n4_list = load_list(n4, "n4_list")

        key_scales_picked = mx_tile(H, U8, "key_scales_picked")
        nc.vector.tensor_copy(key_scales_picked[:], d_scale_table[:].indirect(k1_list[:]))
        key_scales_dealt = mx_tile(H, U8, "key_scales_dealt")
        nc.vector.tensor_copy(
            key_scales_dealt[:].rearrange("p (t m) -> p t m", t=PACK),
            key_scales_picked[:].rearrange("p (m t) -> p t m", t=PACK),
        )
        key_scales = mx_tile(H, U8, "key_scales")
        nc.vector.tensor_copy(key_scales[:].bitcast(I32), key_scales_dealt[:].bitcast(I32))
        for c in range(2):
            nc.scalar.dma_start(
                key_scales[:].bitcast(I32)[2 + c : P : 32, :],
                key_scales_dealt[:].bitcast(I32)[16 + c : P : 32, :],
            )

        key_words_picked = mx_tile(H, U32, "key_words_picked")
        nc.vector.tensor_copy(key_words_picked[:], d_table[:].indirect(k1_list[:]))
        key_words = mx_tile(H, U32, "key_words")
        nc.vector.tensor_copy(
            key_words[:].rearrange("p (t m) -> p m t", t=PACK),
            key_words_picked[:].rearrange("p (m t) -> p m t", t=PACK),
        )
        xq_scales = mx_tile(S, U8, "xq_scales")
        nc.vector.tensor_copy(xq_scales[:], x_scale_table[:].indirect(offs_list[:]))
        xq_words = mx_tile(S, U32, "xq_words")
        nc.vector.tensor_copy(xq_words[:], x_table[:].indirect(offs_list[:]))
        x2_scales = mx_tile(S, U8, "x2_scales")
        nc.vector.tensor_copy(x2_scales[:], x_scale_table[:].indirect(two_list[:]))

        s_banks = [psum.tile([P, S], F32, name=f"s_bank{t}") for t in range(PACK)]
        h_banks = [psum.tile([P, S], F32, name=f"h_bank{t}") for t in range(PACK)]
        for t in range(PACK):
            rows = slice(P * t, P * (t + 1))
            nc.tensor.matmul_mx(
                out=s_banks[t][:], lhsT=key_words[:, rows].bitcast(FP8X4), lhsT_scale=key_scales[:, rows],
                rhs=xq_words[:].bitcast(FP8X4), rhs_scale=xq_scales[:], start=True, stop=True,
            )

        def planes(name, width=S):
            return [sb.tile([P, width], F32, name=f"{name}{t}") for t in range(PACK)]

        s_win = [
            sb.tile([P, VECTOR_WINDOW if t % 2 == 1 else SCALAR_WINDOW], F32, name=f"s_win{t}") for t in range(PACK)
        ]
        for tile in s_win:
            nc.vector.memset(tile[:, S:], 0.0)
        warm_in = sb.tile([P, 1], F32, name="warm_in")
        warm_out = sb.tile([P, 2], F32, name="warm_out")
        nc.vector.memset(warm_in[:], 1.0)
        nc.scalar.activation(warm_out[:, 0:1], warm_in[:], ACT.Abs_reciprocal_sqrt)

        r_win, h_win, sz_win = planes("r_win", WIDE), planes("h_win", WIDE), planes("sz_win", WIDE)
        s_far = planes("s_far")
        st = [tile[:, S:WIDE] for tile in sz_win]
        st_size = [tile[:, S:WIDE] for tile in h_win]
        root = [tile[:, S:WIDE] for tile in r_win]
        halves = (slice(0, S // 2), slice(S // 2, S))
        z = sb.tile([P, PACK, S], F32, name="z")
        x2_words = mx_tile(S, U32, "x2_words")
        nc.vector.tensor_copy(x2_words[:], x_table[:].indirect(two_list[:]))

        for t in range(PACK):
            if t == S_COPY_ON_VECTOR:
                nc.vector.tensor_scalar(s_win[t][:, 0:S], s_banks[t][:], S_SCALE, None, ALU.mult)
            else:
                nc.scalar.activation(s_win[t][:, 0:S], s_banks[t][:], ACT.Copy, scale=S_SCALE)
            if t % 2 == 1:
                nc.vector.tensor_copy(s_far[t][:], s_win[t][:].indirect(n1_list[:]))
            else:
                nc.scalar.activation(s_far[t][:], s_win[t][:].indirect(n1_list[:]), ACT.Copy)
            nc.vector.scalar_tensor_tensor(st[t], s_banks[t][:], S_SCALE, s_far[t][:], ALU.mult, ALU.subtract)
            nc.scalar.activation(st_size[t], st[t], ACT.Abs)
            nc.scalar.activation(root[t], st_size[t], ACT.Abs_reciprocal_sqrt, bias=0.5)
            gain = gn_cols[:, t : t + 1]
            if t < PACK - 1:
                nc.vector.scalar_tensor_tensor(r_win[t][:, 0:S], root[t], gain, root[t], ALU.mult, ALU.mult)
                nc.vector.tensor_tensor(z[:, t, :], r_win[t][:].indirect(n2_list[:]), st[t], ALU.mult)
            else:
                r_far = sb.tile([P, S], F32, name="r_far")
                nc.scalar.activation(r_win[t][:, 0:S], root[t], ACT.Square)
                nc.scalar.activation(r_far[:], r_win[t][:].indirect(n2_list[:]), ACT.Copy)
                for cols in halves:
                    nc.vector.scalar_tensor_tensor(
                        z[:, t, cols], r_far[:, cols], gain, st[t][:, cols], ALU.mult, ALU.mult
                    )

        w_words = mx_tile(2 * N, U32, "w_words")
        for matrix in (slice(N, 2 * N), slice(0, N)):
            nc.gpsimd.tensor_copy(
                w_words[:, matrix].rearrange("p (t m) -> p t m", t=PACK),
                w_word_rows[:, matrix].rearrange("p (m t) -> p t m", t=PACK),
            )
        w_scales = mx_tile(N, U8, "w_scales")
        nc.gpsimd.tensor_copy(
            w_scales[:].rearrange("p (t m) -> p t m", t=PACK),
            w_scale_rows[:].rearrange("p (m t) -> p t m", t=PACK),
        )
        minus_tau = sb.tile([P, PACK], F32, name="minus_tau")
        nc.vector.tensor_scalar(minus_tau[:], tau_cols[:], -1.0, None, ALU.mult)
        for t in range(PACK):
            nc.tensor.matmul_mx(
                out=h_banks[t][:], lhsT=w_words[:, N + P * t : N + P * (t + 1)].bitcast(FP8X4),
                lhsT_scale=w_scales[W2_ROW:P, P * t : P * (t + 1)],
                rhs=x2_words[:].bitcast(FP8X4), rhs_scale=x2_scales[:], start=True, stop=False,
            )
        nc.scalar.activation(warm_out[:, 1:2], r_far[:, 0:1], ACT.Exp)

        def interleave(engine_copy, rounded, values, cols):
            engine_copy(
                rounded[:, cols, :].rearrange("p (c i) t -> p c t i", i=4),
                values[:, :, cols].rearrange("p t (c i) -> p c t i", i=4),
            )

        def quantize(words, scales, rounded, cols):
            nc.vector.quantize_mx(
                out=words[:, cols].bitcast(FP8X4), scales=scales[:, cols],
                in_=rounded[:, cols, :].rearrange("p j t -> p (j t)"),
            )

        z_rounded = sb.tile([P, S, PACK], BF16, name="z_rounded", align_bytes=64)
        z_words, z_scales = mx_tile(S, U32, "z_words"), mx_tile(S, U8, "z_scales")
        for cols in halves:
            interleave(nc.vector.tensor_copy, z_rounded, z, cols)
        for cols in halves:
            quantize(z_words, z_scales, z_rounded, cols)
        for t in range(PACK):
            rows = slice(P * t, P * (t + 1))
            for cols in halves:
                nc.tensor.matmul_mx(
                    out=h_banks[t][:, cols], lhsT=w_words[:, rows].bitcast(FP8X4), lhsT_scale=w_scales[:, rows],
                    rhs=z_words[:, cols].bitcast(FP8X4), rhs_scale=z_scales[:, cols],
                    start=False, stop=(cols == halves[1]),
                )

        h_far, h_diff, ea = planes("h_far"), planes("h_diff"), planes("ea")
        y = sb.tile([P, PACK, S], F32, name="y")
        out_rows = out_0.rearrange("(p t) j -> p t j", t=PACK)

        def copy_out(t):
            if t == H_COPY_ON_VECTOR:
                nc.vector.tensor_copy(h_win[t][:, 0:S], h_banks[t][:])
            else:
                nc.scalar.activation(h_win[t][:, 0:S], h_banks[t][:], ACT.Copy)

        def fetch(t):
            nc.vector.tensor_copy(h_far[t][:], h_win[t][:].indirect(n4_list[:]))

        def size(t):
            nc.scalar.activation(sz_win[t][:, 0:S], h_banks[t][:], ACT.Abs)

        def decay(t):
            nc.scalar.activation(ea[t][:], sz_win[t][:].indirect(n3_list[:]), ACT.Exp, scale=minus_tau[:, t : t + 1])

        def differ(t):
            nc.vector.tensor_tensor(h_diff[t][:], h_banks[t][:], h_far[t][:], ALU.subtract)

        def finish(t):
            engine = nc.gpsimd if t < GPSIMD_PRODUCTS else nc.vector
            engine.tensor_tensor(y[:, t, :], h_diff[t][:], ea[t][:], ALU.mult)
            nc.sync.dma_start(out_rows[:, t, :], y[:, t, :])

        steps = (copy_out, fetch, size, decay, differ, finish)
        for wave in range(len(steps) + PACK - 1):
            for t in range(PACK):
                if 0 <= wave - t < len(steps):
                    steps[wave - t](t)

        y_rounded = sb.tile([P, S, PACK], BF16, name="y_rounded", align_bytes=64)
        y_words, y_scales = mx_tile(S, U32, "y_words"), mx_tile(S, U8, "y_scales")
        interleave(nc.scalar.copy, y_rounded, y, slice(0, SCALAR_ROUND_COLS))
        interleave(nc.vector.tensor_copy, y_rounded, y, slice(SCALAR_ROUND_COLS, S))
        quantize(y_words, y_scales, y_rounded, slice(0, S))
        nc.sync.dma_start(as_words(out_1), y_words[:].bitcast(I32))
        for q in range(QUADRANTS):
            queue = nc.scalar if q % 2 == 0 else nc.sync
            queue.dma_start(
                out_2[0].bitcast(I32)[4 * q : 4 * q + 4, :], y_scales[:].bitcast(I32)[32 * q : 32 * q + 4, :]
            )
